import numpy as np
import ml_dtypes


def mxq(x, axis, fmt="e4m3"):
    dtype, down = {"e4m3": (ml_dtypes.float8_e4m3fn, 7), "e5m2": (ml_dtypes.float8_e5m2, 14)}[fmt]
    v = np.moveaxis(np.asarray(x, np.float32).astype(ml_dtypes.bfloat16).astype(np.float64), axis, -1)
    blocks = v.reshape(v.shape[:-1] + (-1, 32))
    amax = np.abs(blocks).max(-1, keepdims=True)
    byte = np.maximum(np.where(amax > 0, np.frexp(amax)[1] - 1 + 127, 0) - down, 1)
    scale = np.exp2(byte - 127.0)
    codes = (blocks / scale).astype(np.float32).astype(dtype).astype(np.float64)
    return np.moveaxis((codes * scale).reshape(v.shape), -1, axis)


WIDE = False


def mx_kscale(k):
    if not WIDE:
        return np.ones(k)
    levels = np.array([10, -10, 5, -5, 0])
    if k % 512:
        return np.exp2(np.random.permutation(np.resize(levels, k // 32))).repeat(32)
    a = np.empty((k // 512, 16))
    for p in range(k // 512):
        a[p, :8] = np.random.permutation(np.resize(levels, 8))
        for g in range(8):
            far = levels[np.abs(levels - a[p, g]) >= 10]
            a[p, g + 8] = far[np.random.randint(len(far))]
    return np.exp2(a.ravel()).repeat(32)


def f64(x):
    return np.asarray(x).astype(np.float64)


def striped(idx):
    return np.tile(idx.reshape(-1, 16).T, (8, 1)).astype(np.uint16)


def unstriped(offs):
    return offs[:16].T.reshape(-1).astype(np.int64)


def striped8(idx):
    return np.concatenate([x.reshape(-1, 16).T for x in idx]).astype(np.uint16)


def runs(offs, k):
    lists = np.stack([offs[16 * r : 16 * r + 16].T.reshape(-1) for r in range(8)]).astype(np.int64)
    return lists[np.arange(k) % 512 // 64]


def pack_weight(w):
    k, n = w.shape
    w = f64(np.asarray(w, np.float32).astype(ml_dtypes.bfloat16)).reshape(k // 32, 32, n)
    amax = np.abs(w).max(1)
    byte = np.clip(np.where(amax > 0, np.frexp(amax)[1] - 1 + 127 - 7, 1), 1, 254)
    scaled = (w * np.exp2(127.0 - byte)[:, None, :]).reshape(k, n).astype(np.float32)
    words = np.ascontiguousarray(scaled.reshape(k // 512, 128, 4, n).transpose(0, 1, 3, 2)).astype(ml_dtypes.float8_e4m3fn).view(np.uint8)
    return words, np.ascontiguousarray(byte.astype(np.uint8).reshape(k // 512, 16, n))


def unpack_weight(words, scales):
    g, p, n, _ = words.shape
    vals = np.ascontiguousarray(words).view(ml_dtypes.float8_e4m3fn).astype(np.float64) * np.repeat(np.exp2(scales.astype(np.float64) - 127.0), 8, axis=1)[..., None]
    return vals.transpose(0, 1, 3, 2).reshape(g * 512, n)


def sigmoid(v):
    return 1.0 / (1.0 + np.exp(-np.maximum(v, -700.0)))


K, T, S, V, G, H = 512, 2048, 1024, 512, 2048, 512


def setup_inputs():
    n = np.random.standard_normal
    s = mx_kscale(K)[:, None]
    packed_xT = pack_weight(n((K, T)) * s)
    packed_dT = pack_weight(n((K, G)) / s)
    return {
        "x_words": packed_xT[0],
        "x_scales": packed_xT[1],
        "d_words": packed_dT[0],
        "d_scales": packed_dT[1],
        "gs": (np.random.uniform(0.5, 1.5, (K, 1)) * s).astype(np.float32),
        "offs": striped(np.random.permutation(T)[:S]),
        "k1": striped8(np.random.randint(0, G, (8, H))),
        "n1": striped8(np.stack([np.random.permutation(S) for _ in range(8)])),
        "n2": striped8(np.stack([np.random.permutation(V) for _ in range(8)])),
        "n3": striped8(np.stack([np.random.permutation(V) for _ in range(8)])),
    }


def reference(x_words, x_scales, d_words, d_scales, gs, offs, k1, n1, n2, n3):
    d_k1 = unpack_weight(d_words, d_scales)[np.arange(K)[:, None], runs(k1, K)]
    xq = unpack_weight(x_words, x_scales)[:, unstriped(offs)]
    h = 0.0625 * (d_k1.T @ xq)
    ln = h[np.arange(H)[:, None], runs(n1, H)]
    mx = ln.reshape(H, V, 2).max(axis=2)
    mn = ln.reshape(H, V, 2).min(axis=2)
    z = f64(gs) * (mx - (0.5 * mn))
    h2 = 0.0625 * ((d_k1.T @ mxq(z, 0, "e4m3")))
    return h2 + (sigmoid(h2[np.arange(H)[:, None], runs(n2, H)])) * (h2[np.arange(H)[:, None], runs(n3, H)] - h2)

@@ -1,0 +1,179 @@
+from contextlib import ExitStack
+
+import concourse.mybir as mybir
+
+K, T, S, V, G, H = 512, 2048, 1024, 512, 2048, 512
+FLOPS = 2 * K * H * (S + V)
+
+F32 = mybir.dt.float32
+BF16 = mybir.dt.bfloat16
+I32 = mybir.dt.int32
+U32 = mybir.dt.uint32
+U16 = mybir.dt.uint16
+U8 = mybir.dt.uint8
+FP8X4 = mybir.dt.float8_e4m3fn_x4
+ALU = mybir.AluOpType
+ACT = mybir.ActivationFunctionType
+
+P = 128
+PACK = 4
+BANK = 512
+SIXTEENTH = 0.0625
+PAIR_CHUNKS = (256, 128, 128)
+HALF = V // 2
+
+
+def entries(lists, first, count):
+    return lists[:, first // 16 : (first + count) // 16]
+
+
+def tile_picked_ringpgaptrack_none_p_kernel(tc, x_words, x_scales, d_words, d_scales, gs, offs, k1, n1, n2, n3, out):
+    nc = tc.nc
+    with ExitStack() as ctx:
+        keep = ctx.enter_context(tc.tile_pool(name="keep", bufs=1))
+        psum = ctx.enter_context(tc.psum_pool(name="psum", bufs=1))
+
+        k1_t = keep.tile([P, H // 16], U16, name="k1_t")
+        offs_t = keep.tile([P, S // 16], U16, name="offs_t")
+        n1_t = keep.tile([P, S // 16], U16, name="n1_t")
+        n2_t = keep.tile([P, V // 16], U16, name="n2_t")
+        n3_t = keep.tile([P, V // 16], U16, name="n3_t")
+        gain = keep.tile([P, PACK], F32, name="gain")
+        d_bytes = keep.tile([P, G], U8, name="d_bytes", align_bytes=64)
+        x_bytes = keep.tile([P, T], U8, name="x_bytes", align_bytes=64)
+        d_table = keep.tile([P, G], U32, name="d_table", align_bytes=64)
+        x_table = keep.tile([P, T], U32, name="x_table", align_bytes=64)
+        w_scales = keep.tile([P, H], U8, name="w_scales", align_bytes=64)
+
+        nc.gpsimd.memset(d_bytes[:].bitcast(I32), 0)
+        nc.vector.memset(x_bytes[:].bitcast(I32), 0)
+        nc.gpsimd.memset(w_scales[:].bitcast(I32), 0)
+        warm_in = keep.tile([P, 1], F32, name="warm_in")
+        warm_out = keep.tile([P, 1], F32, name="warm_out")
+        nc.gpsimd.memset(warm_in[:], 0.0)
+        nc.scalar.activation(warm_out[:], warm_in[:], ACT.Sigmoid)
+
+        nc.sync.dma_start(k1_t[:], k1)
+        nc.sync.dma_start(d_bytes[:].bitcast(I32)[0:P:8, :], d_scales[0].bitcast(I32))
+        nc.sync.dma_start(offs_t[:], offs)
+        for q in range(4):
+            nc.sync.dma_start(x_bytes[:].bitcast(I32)[32 * q : 32 * q + 4, :], x_scales[0, 4 * q : 4 * q + 4, :].bitcast(I32))
+        nc.sync.dma_start(d_table[:].bitcast(I32), d_words[0].rearrange("p n t -> p (n t)").bitcast(I32))
+        nc.sync.dma_start(x_table[:].bitcast(I32), x_words[0].rearrange("p n t -> p (n t)").bitcast(I32))
+        nc.sync.dma_start(n1_t[:], n1)
+
+        picked_d_bytes = keep.tile([P, H], U8, name="picked_d_bytes", align_bytes=64)
+        nc.vector.tensor_copy(picked_d_bytes[:], d_bytes[:].indirect(k1_t[:]))
+        dealt_d_bytes = keep.tile([P, H], U8, name="dealt_d_bytes", align_bytes=64)
+        nc.vector.tensor_copy(
+            dealt_d_bytes[:].rearrange("p (t m) -> p m t", t=PACK), picked_d_bytes[:].rearrange("p (m t) -> p m t", t=PACK)
+        )
+        for j in range(4):
+            nc.scalar.dma_start(w_scales[:].bitcast(I32)[j:P:32, :], dealt_d_bytes[:].bitcast(I32)[8 * j : P : 32, :])
+
+        nc.sync.dma_start(gain[:], gs.rearrange("(p t) o -> p (t o)", t=PACK))
+        nc.sync.dma_start(n2_t[:], n2)
+        nc.sync.dma_start(n3_t[:], n3)
+
+        xq_scales = keep.tile([P, S], U8, name="xq_scales", align_bytes=64)
+        nc.vector.tensor_copy(xq_scales[:], x_bytes[:].indirect(offs_t[:]))
+
+        picked_d_words = keep.tile([P, H], U32, name="picked_d_words", align_bytes=64)
+        nc.vector.tensor_copy(picked_d_words[:], d_table[:].indirect(k1_t[:]))
+        w_words = keep.tile([P, H], U32, name="w_words", align_bytes=64)
+        nc.vector.tensor_copy(
+            w_words[:].rearrange("p (t m) -> p m t", t=PACK), picked_d_words[:].rearrange("p (m t) -> p m t", t=PACK)
+        )
+
+        def product(bank, t, codes, scales):
+            cols = slice(P * t, P * (t + 1))
+            nc.tensor.matmul_mx(
+                bank, lhsT=w_words[:, cols].bitcast(FP8X4), lhsT_scale=w_scales[:, cols],
+                rhs=codes.bitcast(FP8X4), rhs_scale=scales, start=True, stop=True,
+            )
+
+        h = [keep.tile([P, S], F32, name=f"h{t}", align_bytes=64) for t in range(PACK)]
+        h_banks = {}
+        for b in range(S // BANK):
+            xq_words = keep.tile([P, BANK], U32, name=f"xq_words{b}", align_bytes=64)
+            nc.vector.tensor_copy(xq_words[:], x_table[:].indirect(entries(offs_t, BANK * b, BANK)))
+            for t in range(PACK):
+                h_banks[t, b] = psum.tile([P, BANK], F32, name=f"h_bank{t}_{b}", tag=f"bank{2 * t + b}")
+                product(h_banks[t, b][:], t, xq_words[:], xq_scales[:, BANK * b : BANK * (b + 1)])
+        for t, b in ((0, 0), (1, 0), (0, 1), (1, 1), (2, 0), (2, 1), (3, 0), (3, 1)):
+            nc.scalar.activation(h[t][:, BANK * b : BANK * (b + 1)], h_banks[t, b][:], ACT.Copy, scale=SIXTEENTH)
+
+        h2 = [keep.tile([P, V], F32, name=f"h2_{t}", align_bytes=64) for t in range(PACK)]
+        h2_banks = [psum.tile([P, V], F32, name=f"h2_bank{t}", tag=f"bank{2 * t}") for t in range(PACK)]
+
+        def line_up(c, first, n):
+            lined = keep.tile([P, PACK, 2 * n], F32, name=f"lined{c}", tag="lined", align_bytes=64)
+            for t in range(PACK):
+                nc.vector.tensor_copy(lined[:, t, :], h[t][:].indirect(entries(n1_t, 2 * first, 2 * n)))
+            pairs = lined[:].rearrange("p t (v e) -> p (t v) e", e=2)
+            larger = keep.tile([P, PACK * n], F32, name=f"larger{c}", align_bytes=64)
+            smaller = keep.tile([P, PACK * n], F32, name=f"smaller{c}", align_bytes=64)
+            gap = keep.tile([P, PACK * n], F32, name=f"gap{c}", align_bytes=64)
+            nc.vector.tensor_tensor(larger[:], pairs[:, :, 0], pairs[:, :, 1], ALU.max)
+            nc.vector.tensor_tensor(smaller[:], pairs[:, :, 0], pairs[:, :, 1], ALU.min)
+            nc.vector.scalar_tensor_tensor(gap[:], smaller[:], -0.5, larger[:], ALU.mult, ALU.add)
+            z = keep.tile([P, PACK * n], BF16, name=f"z{c}", align_bytes=64)
+            woven = z[:].rearrange("p (c i t) -> p c t i", i=4, t=PACK)
+            if first + n == V:
+                nc.vector.tensor_tensor(
+                    woven,
+                    gap[:].rearrange("p (t c i) -> p c t i", t=PACK, i=4),
+                    gain[:].rearrange("p (c t i) -> p c t i", c=1, i=1).to_broadcast([P, n // 4, PACK, 4]),
+                    ALU.mult,
+                )
+            else:
+                planes = keep.tile([P, PACK * n], BF16, name=f"planes{c}", align_bytes=64)
+                for t in range(PACK):
+                    nc.scalar.activation(planes[:, n * t : n * (t + 1)], gap[:, n * t : n * (t + 1)], ACT.Copy, scale=gain[:, t : t + 1])
+                nc.scalar.copy(woven, planes[:].rearrange("p (t c i) -> p c t i", t=PACK, i=4))
+            return z
+
+        def second_product(c, first, n, z):
+            z_words = keep.tile([P, n], U32, name=f"z_words{c}", align_bytes=64)
+            z_scales = keep.tile([P, n], U8, name=f"z_scales{c}", align_bytes=64)
+            nc.vector.quantize_mx(z_words[:].bitcast(FP8X4), z_scales[:], z[:])
+            cols = slice(first, first + n)
+            for t in range(PACK):
+                product(h2_banks[t][:, cols], t, z_words[:], z_scales[:])
+            for t in range(PACK):
+                if first + n == V and t > 0:
+                    nc.vector.tensor_scalar(h2[t][:, cols], h2_banks[t][:, cols], SIXTEENTH, None, ALU.mult)
+                else:
+                    nc.scalar.activation(h2[t][:, cols], h2_banks[t][:, cols], ACT.Copy, scale=SIXTEENTH)
+
+        first = 0
+        waiting = None
+        for c, n in enumerate(PAIR_CHUNKS):
+            z = line_up(c, first, n)
+            if waiting is not None:
+                second_product(*waiting)
+            waiting = (c, first, n, z)
+            first = first + n
+        second_product(*waiting)
+
+        out_rows = out.rearrange("(p t) v -> p t v", t=PACK)
+        for t in range(PACK):
+            gate = keep.tile([P, V], F32, name=f"gate{t}", align_bytes=64)
+            near = keep.tile([P, V], F32, name=f"near{t}", align_bytes=64)
+            far = keep.tile([P, V], F32, name=f"far{t}", align_bytes=64)
+            result = keep.tile([P, V], F32, name=f"result{t}", align_bytes=64)
+            for v0 in range(0, V, HALF):
+                cols = slice(v0, v0 + HALF)
+                nc.scalar.activation(gate[:, cols], h2[t][:].indirect(entries(n2_t, v0, HALF)), ACT.Sigmoid)
+            width = HALF if t in (0, PACK - 1) else V
+            for v0 in range(0, V, HALF):
+                cols = slice(v0, v0 + HALF)
+                nc.vector.tensor_tensor(far[:, cols], h2[t][:].indirect(entries(n3_t, v0, HALF)), gate[:, cols], ALU.mult)
+                if (v0 + HALF) % width == 0:
+                    cols = slice(v0 + HALF - width, v0 + HALF)
+                    nc.vector.scalar_tensor_tensor(near[:, cols], gate[:, cols], 1.0, h2[t][:, cols], ALU.subtract, ALU.mult)
+            width = HALF if t == PACK - 1 else V
+            for v0 in range(0, V, width):
+                cols = slice(v0, v0 + width)
+                nc.vector.tensor_tensor(result[:, cols], far[:, cols], near[:, cols], ALU.subtract)
+                nc.sync.dma_start(out_rows[:, t, cols], result[:, cols])

@@ -48,10 +48,6 @@ def tile_picked_ringpgaptrack_none_p_kernel(tc, x_words, x_scales, d_words, d_sc
         nc.gpsimd.memset(d_bytes[:].bitcast(I32), 0)
         nc.vector.memset(x_bytes[:].bitcast(I32), 0)
         nc.gpsimd.memset(w_scales[:].bitcast(I32), 0)
-        warm_in = keep.tile([P, 1], F32, name="warm_in")
-        warm_out = keep.tile([P, 1], F32, name="warm_out")
-        nc.gpsimd.memset(warm_in[:], 0.0)
-        nc.scalar.activation(warm_out[:], warm_in[:], ACT.Sigmoid)
 
         nc.sync.dma_start(k1_t[:], k1)
         nc.sync.dma_start(d_bytes[:].bitcast(I32)[0:P:8, :], d_scales[0].bitcast(I32))
@@ -75,9 +71,6 @@ def tile_picked_ringpgaptrack_none_p_kernel(tc, x_words, x_scales, d_words, d_sc
         nc.sync.dma_start(n2_t[:], n2)
         nc.sync.dma_start(n3_t[:], n3)
 
-        xq_scales = keep.tile([P, S], U8, name="xq_scales", align_bytes=64)
-        nc.vector.tensor_copy(xq_scales[:], x_bytes[:].indirect(offs_t[:]))
-
         picked_d_words = keep.tile([P, H], U32, name="picked_d_words", align_bytes=64)
         nc.vector.tensor_copy(picked_d_words[:], d_table[:].indirect(k1_t[:]))
         w_words = keep.tile([P, H], U32, name="w_words", align_bytes=64)
@@ -92,31 +85,40 @@ def tile_picked_ringpgaptrack_none_p_kernel(tc, x_words, x_scales, d_words, d_sc
                 rhs=codes.bitcast(FP8X4), rhs_scale=scales, start=True, stop=True,
             )
 
+        xq_scales = keep.tile([P, S], U8, name="xq_scales", align_bytes=64)
+        xq_words = keep.tile([P, S], U32, name="xq_words", align_bytes=64)
         h = [keep.tile([P, S], F32, name=f"h{t}", align_bytes=64) for t in range(PACK)]
-        h_banks = {}
-        for b in range(S // BANK):
-            xq_words = keep.tile([P, BANK], U32, name=f"xq_words{b}", align_bytes=64)
-            nc.vector.tensor_copy(xq_words[:], x_table[:].indirect(entries(offs_t, BANK * b, BANK)))
-            for t in range(PACK):
-                h_banks[t, b] = psum.tile([P, BANK], F32, name=f"h_bank{t}_{b}", tag=f"bank{2 * t + b}")
-                product(h_banks[t, b][:], t, xq_words[:], xq_scales[:, BANK * b : BANK * (b + 1)])
-        for t, b in ((0, 0), (1, 0), (0, 1), (1, 1), (2, 0), (2, 1), (3, 0), (3, 1)):
-            nc.scalar.activation(h[t][:, BANK * b : BANK * (b + 1)], h_banks[t, b][:], ACT.Copy, scale=SIXTEENTH)
+
+        def pick_x(table, picked, first, n):
+            nc.vector.tensor_copy(picked[:, first : first + n], table[:].indirect(entries(offs_t, first, n)))
+
+        pick_x(x_bytes, xq_scales, 0, 512)
+        pick_x(x_table, xq_words, 0, 512)
+        pick_x(x_bytes, xq_scales, 512, 512)
+        pick_x(x_table, xq_words, 512, 256)
+        pick_x(x_table, xq_words, 768, 256)
+        steps = ((0, 0, 512), (1, 0, 512), (0, 512, 256), (0, 768, 256), (1, 512, 512), (2, 0, 512), (2, 512, 512), (3, 0, 512), (3, 512, 512))
+        for i, (t, first, n) in enumerate(steps):
+            bank = psum.tile([P, n], F32, name=f"h_bank{i}", tag=f"bank{i % 8}")
+            cols = slice(first, first + n)
+            product(bank[:], t, xq_words[:, cols], xq_scales[:, cols])
+            nc.scalar.activation(h[t][:, cols], bank[:], ACT.Copy, scale=SIXTEENTH / 2)
 
         h2 = [keep.tile([P, V], F32, name=f"h2_{t}", align_bytes=64) for t in range(PACK)]
-        h2_banks = [psum.tile([P, V], F32, name=f"h2_bank{t}", tag=f"bank{2 * t}") for t in range(PACK)]
+        h2_banks = [psum.tile([P, V], F32, name=f"h2_bank{t}", tag=f"bank{t + 1}") for t in range(PACK)]
 
         def line_up(c, first, n):
-            lined = keep.tile([P, PACK, 2 * n], F32, name=f"lined{c}", tag="lined", align_bytes=64)
-            for t in range(PACK):
-                nc.vector.tensor_copy(lined[:, t, :], h[t][:].indirect(entries(n1_t, 2 * first, 2 * n)))
-            pairs = lined[:].rearrange("p t (v e) -> p (t v) e", e=2)
+            lined = keep.tile([P, PACK * 2 * n], F32, name=f"lined{c}", tag="lined", align_bytes=64)
+            pairs = lined[:].rearrange("p (v e) -> p v e", e=2)
+            both = keep.tile([P, PACK * n], F32, name=f"both{c}", align_bytes=64)
             larger = keep.tile([P, PACK * n], F32, name=f"larger{c}", align_bytes=64)
-            smaller = keep.tile([P, PACK * n], F32, name=f"smaller{c}", align_bytes=64)
             gap = keep.tile([P, PACK * n], F32, name=f"gap{c}", align_bytes=64)
+            for t in range(PACK):
+                nc.vector.tensor_copy(lined[:, 2 * n * t : 2 * n * (t + 1)], h[t][:].indirect(entries(n1_t, 2 * first, 2 * n)))
+                cols = slice(n * t, n * (t + 1))
+                nc.gpsimd.tensor_tensor(both[:, cols], pairs[:, cols, 0], pairs[:, cols, 1], ALU.add)
             nc.vector.tensor_tensor(larger[:], pairs[:, :, 0], pairs[:, :, 1], ALU.max)
-            nc.vector.tensor_tensor(smaller[:], pairs[:, :, 0], pairs[:, :, 1], ALU.min)
-            nc.vector.scalar_tensor_tensor(gap[:], smaller[:], -0.5, larger[:], ALU.mult, ALU.add)
+            nc.vector.scalar_tensor_tensor(gap[:], larger[:], 3.0, both[:], ALU.mult, ALU.subtract)
             z = keep.tile([P, PACK * n], BF16, name=f"z{c}", align_bytes=64)
             woven = z[:].rearrange("p (c i t) -> p c t i", i=4, t=PACK)
             if first + n == V:
@@ -141,7 +143,7 @@ def tile_picked_ringpgaptrack_none_p_kernel(tc, x_words, x_scales, d_words, d_sc
             for t in range(PACK):
                 product(h2_banks[t][:, cols], t, z_words[:], z_scales[:])
             for t in range(PACK):
-                if first + n == V and t > 0:
+                if first + n == V:
                     nc.vector.tensor_scalar(h2[t][:, cols], h2_banks[t][:, cols], SIXTEENTH, None, ALU.mult)
                 else:
                     nc.scalar.activation(h2[t][:, cols], h2_banks[t][:, cols], ACT.Copy, scale=SIXTEENTH)

@@ -45,9 +45,9 @@ def tile_picked_ringpgaptrack_none_p_kernel(tc, x_words, x_scales, d_words, d_sc
         x_table = keep.tile([P, T], U32, name="x_table", align_bytes=64)
         w_scales = keep.tile([P, H], U8, name="w_scales", align_bytes=64)
 
-        nc.gpsimd.memset(d_bytes[:].bitcast(I32), 0)
+        nc.vector.memset(d_bytes[:].bitcast(I32), 0)
         nc.vector.memset(x_bytes[:].bitcast(I32), 0)
-        nc.gpsimd.memset(w_scales[:].bitcast(I32), 0)
+        nc.vector.memset(w_scales[:].bitcast(I32), 0)
 
         nc.sync.dma_start(k1_t[:], k1)
         nc.sync.dma_start(d_bytes[:].bitcast(I32)[0:P:8, :], d_scales[0].bitcast(I32))
@@ -58,8 +58,15 @@ def tile_picked_ringpgaptrack_none_p_kernel(tc, x_words, x_scales, d_words, d_sc
         nc.sync.dma_start(x_table[:].bitcast(I32), x_words[0].rearrange("p n t -> p (n t)").bitcast(I32))
         nc.sync.dma_start(n1_t[:], n1)
 
+        xq_scales = keep.tile([P, S], U8, name="xq_scales", align_bytes=64)
+        xq_words = keep.tile([P, S], U32, name="xq_words", align_bytes=64)
+
+        def pick_x(table, picked, first, n):
+            nc.vector.tensor_copy(picked[:, first : first + n], table[:].indirect(entries(offs_t, first, n)))
+
         picked_d_bytes = keep.tile([P, H], U8, name="picked_d_bytes", align_bytes=64)
         nc.vector.tensor_copy(picked_d_bytes[:], d_bytes[:].indirect(k1_t[:]))
+        pick_x(x_bytes, xq_scales, 0, 512)
         dealt_d_bytes = keep.tile([P, H], U8, name="dealt_d_bytes", align_bytes=64)
         nc.vector.tensor_copy(
             dealt_d_bytes[:].rearrange("p (t m) -> p m t", t=PACK), picked_d_bytes[:].rearrange("p (m t) -> p m t", t=PACK)
@@ -73,6 +80,7 @@ def tile_picked_ringpgaptrack_none_p_kernel(tc, x_words, x_scales, d_words, d_sc
 
         picked_d_words = keep.tile([P, H], U32, name="picked_d_words", align_bytes=64)
         nc.vector.tensor_copy(picked_d_words[:], d_table[:].indirect(k1_t[:]))
+        pick_x(x_bytes, xq_scales, 512, 512)
         w_words = keep.tile([P, H], U32, name="w_words", align_bytes=64)
         nc.vector.tensor_copy(
             w_words[:].rearrange("p (t m) -> p m t", t=PACK), picked_d_words[:].rearrange("p (m t) -> p m t", t=PACK)
@@ -85,49 +93,66 @@ def tile_picked_ringpgaptrack_none_p_kernel(tc, x_words, x_scales, d_words, d_sc
                 rhs=codes.bitcast(FP8X4), rhs_scale=scales, start=True, stop=True,
             )
 
-        xq_scales = keep.tile([P, S], U8, name="xq_scales", align_bytes=64)
-        xq_words = keep.tile([P, S], U32, name="xq_words", align_bytes=64)
         h = [keep.tile([P, S], F32, name=f"h{t}", align_bytes=64) for t in range(PACK)]
-
-        def pick_x(table, picked, first, n):
-            nc.vector.tensor_copy(picked[:, first : first + n], table[:].indirect(entries(offs_t, first, n)))
-
-        pick_x(x_bytes, xq_scales, 0, 512)
         pick_x(x_table, xq_words, 0, 512)
-        pick_x(x_bytes, xq_scales, 512, 512)
         pick_x(x_table, xq_words, 512, 256)
         pick_x(x_table, xq_words, 768, 256)
-        steps = ((0, 0, 512), (1, 0, 512), (0, 512, 256), (0, 768, 256), (1, 512, 512), (2, 0, 512), (2, 512, 512), (3, 0, 512), (3, 512, 512))
+        steps = ((0, 0, 512), (0, 512, 256), (0, 768, 256), (1, 0, 512), (1, 512, 512), (2, 0, 512), (2, 512, 512), (3, 0, 512), (3, 512, 512))
         for i, (t, first, n) in enumerate(steps):
             bank = psum.tile([P, n], F32, name=f"h_bank{i}", tag=f"bank{i % 8}")
             cols = slice(first, first + n)
             product(bank[:], t, xq_words[:, cols], xq_scales[:, cols])
-            nc.scalar.activation(h[t][:, cols], bank[:], ACT.Copy, scale=SIXTEENTH / 2)
+            if i == 2:
+                nc.vector.tensor_scalar(h[t][:, cols], bank[:], SIXTEENTH / 2, None, ALU.mult)
+            else:
+                nc.scalar.activation(h[t][:, cols], bank[:], ACT.Copy, scale=SIXTEENTH / 2)
 
         h2 = [keep.tile([P, V], F32, name=f"h2_{t}", align_bytes=64) for t in range(PACK)]
         h2_banks = [psum.tile([P, V], F32, name=f"h2_bank{t}", tag=f"bank{t + 1}") for t in range(PACK)]
 
-        def line_up(c, first, n):
-            lined = keep.tile([P, PACK * 2 * n], F32, name=f"lined{c}", tag="lined", align_bytes=64)
+        def line_up(c, first, n, tag):
+            lined = keep.tile([P, PACK * 2 * n], F32, name=f"lined{c}", tag=tag, align_bytes=64)
             pairs = lined[:].rearrange("p (v e) -> p v e", e=2)
             both = keep.tile([P, PACK * n], F32, name=f"both{c}", align_bytes=64)
-            larger = keep.tile([P, PACK * n], F32, name=f"larger{c}", align_bytes=64)
-            gap = keep.tile([P, PACK * n], F32, name=f"gap{c}", align_bytes=64)
             for t in range(PACK):
                 nc.vector.tensor_copy(lined[:, 2 * n * t : 2 * n * (t + 1)], h[t][:].indirect(entries(n1_t, 2 * first, 2 * n)))
-                cols = slice(n * t, n * (t + 1))
-                nc.gpsimd.tensor_tensor(both[:, cols], pairs[:, cols, 0], pairs[:, cols, 1], ALU.add)
-            nc.vector.tensor_tensor(larger[:], pairs[:, :, 0], pairs[:, :, 1], ALU.max)
-            nc.vector.scalar_tensor_tensor(gap[:], larger[:], 3.0, both[:], ALU.mult, ALU.subtract)
-            z = keep.tile([P, PACK * n], BF16, name=f"z{c}", align_bytes=64)
+                if t < PACK - 1:
+                    cols = slice(n * t, n * (t + 1))
+                    nc.gpsimd.tensor_tensor(both[:, cols], pairs[:, cols, 0], pairs[:, cols, 1], ALU.add)
+            return pairs, both
+
+        def combine(c, n, pairs, both, larger_tag, last):
+            larger = keep.tile([P, PACK * n], F32, name=f"larger{c}", tag=larger_tag, align_bytes=64)
+            gap = keep.tile([P, PACK * n], F32, name=f"gap{c}", align_bytes=64)
+            head, tail = slice(0, n * (PACK - 1)), slice(n * (PACK - 1), n * PACK)
+            if last:
+                nc.vector.tensor_tensor(both[:, tail], pairs[:, tail, 0], pairs[:, tail, 1], ALU.add)
+                by_plane = pairs.rearrange("p (t v) e -> p t v e", t=PACK)
+                views = [tile[:].rearrange("p (t v) -> p t v", t=PACK) for tile in (larger, both, gap)]
+                halves = (slice(0, n // 2), slice(n // 2, n))
+                for half in halves:
+                    nc.vector.tensor_tensor(views[0][:, :, half], by_plane[:, :, half, 0], by_plane[:, :, half, 1], ALU.max)
+                for half in halves:
+                    nc.vector.scalar_tensor_tensor(views[2][:, :, half], views[0][:, :, half], 3.0, views[1][:, :, half], ALU.mult, ALU.subtract)
+            else:
+                nc.vector.tensor_tensor(larger[:, head], pairs[:, head, 0], pairs[:, head, 1], ALU.max)
+                nc.vector.tensor_tensor(both[:, tail], pairs[:, tail, 0], pairs[:, tail, 1], ALU.add)
+                nc.vector.tensor_tensor(larger[:, tail], pairs[:, tail, 0], pairs[:, tail, 1], ALU.max)
+                for cols in (head, tail):
+                    nc.vector.scalar_tensor_tensor(gap[:, cols], larger[:, cols], 3.0, both[:, cols], ALU.mult, ALU.subtract)
+            return gap
+
+        def weave(c, n, gap, tag, last):
+            z = keep.tile([P, PACK * n], BF16, name=f"z{c}", tag=tag, align_bytes=64)
             woven = z[:].rearrange("p (c i t) -> p c t i", i=4, t=PACK)
-            if first + n == V:
-                nc.vector.tensor_tensor(
-                    woven,
-                    gap[:].rearrange("p (t c i) -> p c t i", t=PACK, i=4),
-                    gain[:].rearrange("p (c t i) -> p c t i", c=1, i=1).to_broadcast([P, n // 4, PACK, 4]),
-                    ALU.mult,
-                )
+            if last:
+                for half in (slice(0, n // 8), slice(n // 8, n // 4)):
+                    nc.vector.tensor_tensor(
+                        woven[:, half, :, :],
+                        gap[:].rearrange("p (t c i) -> p c t i", t=PACK, i=4)[:, half, :, :],
+                        gain[:].rearrange("p (c t i) -> p c t i", c=1, i=1).to_broadcast([P, n // 8, PACK, 4]),
+                        ALU.mult,
+                    )
             else:
                 planes = keep.tile([P, PACK * n], BF16, name=f"planes{c}", align_bytes=64)
                 for t in range(PACK):
@@ -135,47 +160,61 @@ def tile_picked_ringpgaptrack_none_p_kernel(tc, x_words, x_scales, d_words, d_sc
                 nc.scalar.copy(woven, planes[:].rearrange("p (t c i) -> p c t i", t=PACK, i=4))
             return z
 
-        def second_product(c, first, n, z):
+        def second_product(c, first, n, z, pieces):
             z_words = keep.tile([P, n], U32, name=f"z_words{c}", align_bytes=64)
             z_scales = keep.tile([P, n], U8, name=f"z_scales{c}", align_bytes=64)
-            nc.vector.quantize_mx(z_words[:].bitcast(FP8X4), z_scales[:], z[:])
+            w = n // pieces
+            for v0 in range(0, n, w):
+                nc.vector.quantize_mx(z_words[:, v0 : v0 + w].bitcast(FP8X4), z_scales[:, v0 : v0 + w], z[:, PACK * v0 : PACK * (v0 + w)])
             cols = slice(first, first + n)
             for t in range(PACK):
                 product(h2_banks[t][:, cols], t, z_words[:], z_scales[:])
+
+        def empty(first, n):
+            cols = slice(first, first + n)
             for t in range(PACK):
                 if first + n == V:
                     nc.vector.tensor_scalar(h2[t][:, cols], h2_banks[t][:, cols], SIXTEENTH, None, ALU.mult)
                 else:
                     nc.scalar.activation(h2[t][:, cols], h2_banks[t][:, cols], ACT.Copy, scale=SIXTEENTH)
 
-        first = 0
-        waiting = None
-        for c, n in enumerate(PAIR_CHUNKS):
-            z = line_up(c, first, n)
-            if waiting is not None:
-                second_product(*waiting)
-            waiting = (c, first, n, z)
-            first = first + n
-        second_product(*waiting)
+        pairs, both = line_up(0, 0, 256, "a")
+        z0 = weave(0, 256, combine(0, 256, pairs, both, "larger", False), "b", False)
+        pairs, both = line_up(1, 256, 128, "a")
+        z1 = weave(1, 128, combine(1, 128, pairs, both, "larger", False), "c", False)
+        second_product(0, 0, 256, z0, 1)
+        empty(0, 256)
+        pairs, both = line_up(2, 384, 128, "b")
+        second_product(1, 256, 128, z1, 1)
+        empty(256, 128)
+        z2 = weave(2, 128, combine(2, 128, pairs, both, "c", True), "d", True)
+        second_product(2, 384, 128, z2, 2)
+        empty(384, 128)
 
         out_rows = out.rearrange("(p t) v -> p t v", t=PACK)
-        for t in range(PACK):
-            gate = keep.tile([P, V], F32, name=f"gate{t}", align_bytes=64)
-            near = keep.tile([P, V], F32, name=f"near{t}", align_bytes=64)
-            far = keep.tile([P, V], F32, name=f"far{t}", align_bytes=64)
+
+        def finish(t, far, near, width):
             result = keep.tile([P, V], F32, name=f"result{t}", align_bytes=64)
-            for v0 in range(0, V, HALF):
-                cols = slice(v0, v0 + HALF)
-                nc.scalar.activation(gate[:, cols], h2[t][:].indirect(entries(n2_t, v0, HALF)), ACT.Sigmoid)
-            width = HALF if t in (0, PACK - 1) else V
-            for v0 in range(0, V, HALF):
-                cols = slice(v0, v0 + HALF)
-                nc.vector.tensor_tensor(far[:, cols], h2[t][:].indirect(entries(n3_t, v0, HALF)), gate[:, cols], ALU.mult)
-                if (v0 + HALF) % width == 0:
-                    cols = slice(v0 + HALF - width, v0 + HALF)
-                    nc.vector.scalar_tensor_tensor(near[:, cols], gate[:, cols], 1.0, h2[t][:, cols], ALU.subtract, ALU.mult)
-            width = HALF if t == PACK - 1 else V
             for v0 in range(0, V, width):
                 cols = slice(v0, v0 + width)
                 nc.vector.tensor_tensor(result[:, cols], far[:, cols], near[:, cols], ALU.subtract)
                 nc.sync.dma_start(out_rows[:, t, cols], result[:, cols])
+
+        waiting = None
+        for t in range(PACK):
+            gate = keep.tile([P, V], F32, name=f"gate{t}", align_bytes=64)
+            near = keep.tile([P, V], F32, name=f"near{t}", align_bytes=64)
+            far = keep.tile([P, V], F32, name=f"far{t}", align_bytes=64)
+            for v0 in range(0, V, HALF):
+                cols = slice(v0, v0 + HALF)
+                nc.scalar.activation(gate[:, cols], h2[t][:].indirect(entries(n2_t, v0, HALF)), ACT.Sigmoid)
+            if t > 0:
+                nc.vector.scalar_tensor_tensor(near[:], gate[:], 1.0, h2[t][:], ALU.subtract, ALU.mult)
+                finish(*waiting)
+            for v0 in range(0, V, HALF):
+                cols = slice(v0, v0 + HALF)
+                nc.vector.tensor_tensor(far[:, cols], h2[t][:].indirect(entries(n3_t, v0, HALF)), gate[:, cols], ALU.mult)
+                if t == 0:
+                    nc.vector.scalar_tensor_tensor(near[:, cols], gate[:, cols], 1.0, h2[t][:, cols], ALU.subtract, ALU.mult)
+            waiting = (t, far, near, HALF if t == PACK - 1 else V)
+        finish(*waiting)

@@ -1,6 +1,7 @@
 from contextlib import ExitStack
 
 import concourse.mybir as mybir
+from concourse.masks import make_identity
 
 K, T, S, V, G, H = 512, 2048, 1024, 512, 2048, 512
 FLOPS = 2 * K * H * (S + V)
@@ -21,6 +22,7 @@ BANK = 512
 SIXTEENTH = 0.0625
 PAIR_CHUNKS = (256, 128, 128)
 HALF = V // 2
+TURNED = 2
 
 
 def entries(lists, first, count):
@@ -78,7 +80,7 @@ def tile_picked_ringpgaptrack_none_p_kernel(tc, x_words, x_scales, d_words, d_sc
         nc.sync.dma_start(n2_t[:], n2)
         nc.sync.dma_start(n3_t[:], n3)
 
-        picked_d_words = keep.tile([P, H], U32, name="picked_d_words", align_bytes=64)
+        picked_d_words = keep.tile([P, H], U32, name="picked_d_words", tag="picked_d_words", align_bytes=64)
         nc.vector.tensor_copy(picked_d_words[:], d_table[:].indirect(k1_t[:]))
         pick_x(x_bytes, xq_scales, 512, 512)
         w_words = keep.tile([P, H], U32, name="w_words", align_bytes=64)
@@ -93,6 +95,8 @@ def tile_picked_ringpgaptrack_none_p_kernel(tc, x_words, x_scales, d_words, d_sc
                 rhs=codes.bitcast(FP8X4), rhs_scale=scales, start=True, stop=True,
             )
 
+        identity = keep.tile([P, P], F32, name="identity", tag="picked_d_words", align_bytes=64)
+        make_identity(nc, identity[:])
         h = [keep.tile([P, S], F32, name=f"h{t}", align_bytes=64) for t in range(PACK)]
         pick_x(x_table, xq_words, 0, 512)
         pick_x(x_table, xq_words, 512, 256)
@@ -121,100 +125,161 @@ def tile_picked_ringpgaptrack_none_p_kernel(tc, x_words, x_scales, d_words, d_sc
                     nc.gpsimd.tensor_tensor(both[:, cols], pairs[:, cols, 0], pairs[:, cols, 1], ALU.add)
             return pairs, both
 
-        def combine(c, n, pairs, both, larger_tag, last):
-            larger = keep.tile([P, PACK * n], F32, name=f"larger{c}", tag=larger_tag, align_bytes=64)
-            gap = keep.tile([P, PACK * n], F32, name=f"gap{c}", align_bytes=64)
-            head, tail = slice(0, n * (PACK - 1)), slice(n * (PACK - 1), n * PACK)
-            if last:
-                nc.vector.tensor_tensor(both[:, tail], pairs[:, tail, 0], pairs[:, tail, 1], ALU.add)
-                by_plane = pairs.rearrange("p (t v) e -> p t v e", t=PACK)
-                views = [tile[:].rearrange("p (t v) -> p t v", t=PACK) for tile in (larger, both, gap)]
-                halves = (slice(0, n // 2), slice(n // 2, n))
-                for half in halves:
-                    nc.vector.tensor_tensor(views[0][:, :, half], by_plane[:, :, half, 0], by_plane[:, :, half, 1], ALU.max)
-                for half in halves:
-                    nc.vector.scalar_tensor_tensor(views[2][:, :, half], views[0][:, :, half], 3.0, views[1][:, :, half], ALU.mult, ALU.subtract)
+        def empty(t, cols, engine):
+            if engine == "vector":
+                nc.vector.tensor_scalar(h2[t][:, cols], h2_banks[t][:, cols], SIXTEENTH, None, ALU.mult)
             else:
-                nc.vector.tensor_tensor(larger[:, head], pairs[:, head, 0], pairs[:, head, 1], ALU.max)
-                nc.vector.tensor_tensor(both[:, tail], pairs[:, tail, 0], pairs[:, tail, 1], ALU.add)
-                nc.vector.tensor_tensor(larger[:, tail], pairs[:, tail, 0], pairs[:, tail, 1], ALU.max)
-                for cols in (head, tail):
-                    nc.vector.scalar_tensor_tensor(gap[:, cols], larger[:, cols], 3.0, both[:, cols], ALU.mult, ALU.subtract)
-            return gap
+                nc.scalar.activation(h2[t][:, cols], h2_banks[t][:, cols], ACT.Copy, scale=SIXTEENTH)
 
-        def weave(c, n, gap, tag, last):
-            z = keep.tile([P, PACK * n], BF16, name=f"z{c}", tag=tag, align_bytes=64)
-            woven = z[:].rearrange("p (c i t) -> p c t i", i=4, t=PACK)
-            if last:
-                for half in (slice(0, n // 8), slice(n // 8, n // 4)):
-                    nc.vector.tensor_tensor(
-                        woven[:, half, :, :],
-                        gap[:].rearrange("p (t c i) -> p c t i", t=PACK, i=4)[:, half, :, :],
-                        gain[:].rearrange("p (c t i) -> p c t i", c=1, i=1).to_broadcast([P, n // 8, PACK, 4]),
-                        ALU.mult,
-                    )
-            else:
-                planes = keep.tile([P, PACK * n], BF16, name=f"planes{c}", align_bytes=64)
+        def second_product(name, first, z):
+            n = z.shape[1] // PACK
+            z_words = keep.tile([P, n], U32, name=f"z_words{name}", align_bytes=64)
+            z_scales = keep.tile([P, n], U8, name=f"z_scales{name}", align_bytes=64)
+            nc.vector.quantize_mx(z_words[:].bitcast(FP8X4), z_scales[:], z[:])
+            for t in range(PACK):
+                product(h2_banks[t][:, first : first + n], t, z_words[:], z_scales[:])
+
+        def second_chunk(n, pairs, both):
+            m = n // 2
+            halves = (slice(0, m), slice(m, n))
+            tail = slice(n * (PACK - 1), n * PACK)
+            nc.vector.tensor_tensor(both[:, tail], pairs[:, tail, 0], pairs[:, tail, 1], ALU.add)
+            by_plane = pairs.rearrange("p (t v) e -> p t v e", t=PACK)
+            both_planes = both[:].rearrange("p (t v) -> p t v", t=PACK)
+            larger = [keep.tile([P, PACK, m], F32, name=f"larger{i}", align_bytes=64) for i in range(2)]
+            gap = [keep.tile([P, PACK, m], F32, name=f"gap{i}", tag=("gap0", "z0")[i], align_bytes=64) for i in range(2)]
+            z = [keep.tile([P, PACK * m], BF16, name=f"z1_{i}", align_bytes=64) for i in range(2)]
+            for i in range(2):
+                nc.vector.tensor_tensor(larger[i][:], by_plane[:, :, halves[i], 0], by_plane[:, :, halves[i], 1], ALU.max)
+            for i in range(2):
+                nc.vector.scalar_tensor_tensor(gap[i][:], larger[i][:], 3.0, both_planes[:, :, halves[i]], ALU.mult, ALU.subtract)
+            for i in range(2):
+                nc.vector.tensor_tensor(
+                    z[i][:].rearrange("p (c i t) -> p c t i", i=4, t=PACK),
+                    gap[i][:].rearrange("p t (c i) -> p c t i", i=4),
+                    gain[:].rearrange("p (c t i) -> p c t i", c=1, i=1).to_broadcast([P, m // 4, PACK, 4]),
+                    ALU.mult,
+                )
+            for i in range(2):
+                second_product(f"1_{i}", n + m * i, z[i])
+
+        def first_chunk(n):
+            half_gain = keep.tile([P, PACK], F32, name="half_gain")
+            nc.scalar.activation(half_gain[:], gain[:], ACT.Copy, scale=0.5)
+            lined = keep.tile([P, PACK * 2 * n], F32, name="lined0", align_bytes=64)
+            pairs = lined[:].rearrange("p (v e) -> p v e", e=2)
+            spread = keep.tile([P, PACK * n], F32, name="spread", align_bytes=64)
+            sum_banks = [psum.tile([P, BANK], F32, name=f"sum_bank{j}", tag=f"bank{5 + j}") for j in range(n // P)]
+            for t in range(PACK):
+                nc.vector.tensor_copy(lined[:, 2 * n * t : 2 * n * (t + 1)], h[t][:].indirect(entries(n1_t, 0, 2 * n)))
+                cols = slice(n * t, n * (t + 1))
+                apart = keep.tile([P, n], F32, name=f"apart{t}", tag="a" if t == 0 else f"apart{t}", align_bytes=64)
+                nc.gpsimd.tensor_tensor(apart[:], pairs[:, cols, 0], pairs[:, cols, 1], ALU.subtract)
+                nc.scalar.activation(spread[:, cols], apart[:], ACT.Abs, scale=3.0)
+            for t in range(PACK):
+                for j in range(n // P):
+                    cols = slice(n * t + P * j, n * t + P * (j + 1))
+                    for e in range(2):
+                        nc.tensor.matmul(
+                            sum_banks[j][:, P * t : P * (t + 1)], pairs[:, cols, e], identity[:], is_transpose=True,
+                            start=t == 0 and e == 0, stop=False,
+                        )
+                for u in ([t - 1] if 0 < t < PACK - 1 else [t - 1, t] if t > 0 else []):
+                    for j in range(n // P):
+                        cols = slice(n * u + P * j, n * u + P * (j + 1))
+                        nc.tensor.matmul(
+                            sum_banks[j][:, P * u : P * (u + 1)], spread[:, cols], identity[:], is_transpose=True,
+                            start=False, stop=u == PACK - 1,
+                        )
+            turned = keep.tile([P, PACK * n], F32, name="turned_gap", align_bytes=64)
+            back_banks = [psum.tile([P, BANK], F32, name=f"gap_bank{j}", tag=f"bank{(7 + j) % 8}") for j in range(2)]
+            for j in range(n // P):
+                nc.scalar.copy(turned[:, BANK * j : BANK * (j + 1)], sum_banks[j][:])
+            for j in range(n // P):
                 for t in range(PACK):
-                    nc.scalar.activation(planes[:, n * t : n * (t + 1)], gap[:, n * t : n * (t + 1)], ACT.Copy, scale=gain[:, t : t + 1])
-                nc.scalar.copy(woven, planes[:].rearrange("p (t c i) -> p c t i", t=PACK, i=4))
+                    place = n * (t % 2) + P * j
+                    nc.tensor.transpose(back_banks[t // 2][:, place : place + P], turned[:, BANK * j + P * t : BANK * j + P * (t + 1)], identity[:])
+            planes = keep.tile([P, PACK * n], BF16, name="planes0", tag="planes", align_bytes=64)
+            for t in range(PACK):
+                place = n * (t % 2)
+                nc.scalar.activation(planes[:, n * t : n * (t + 1)], back_banks[t // 2][:, place : place + n], ACT.Copy, scale=half_gain[:, t : t + 1])
+            z = keep.tile([P, PACK * n], BF16, name="z0", tag="z0", align_bytes=64)
+            nc.scalar.copy(z[:].rearrange("p (c i t) -> p c t i", i=4, t=PACK), planes[:].rearrange("p (t c i) -> p c t i", t=PACK, i=4))
             return z
 
-        def second_product(c, first, n, z, pieces):
-            z_words = keep.tile([P, n], U32, name=f"z_words{c}", align_bytes=64)
-            z_scales = keep.tile([P, n], U8, name=f"z_scales{c}", align_bytes=64)
-            w = n // pieces
-            for v0 in range(0, n, w):
-                nc.vector.quantize_mx(z_words[:, v0 : v0 + w].bitcast(FP8X4), z_scales[:, v0 : v0 + w], z[:, PACK * v0 : PACK * (v0 + w)])
-            cols = slice(first, first + n)
-            for t in range(PACK):
-                product(h2_banks[t][:, cols], t, z_words[:], z_scales[:])
-
-        def empty(first, n):
-            cols = slice(first, first + n)
-            for t in range(PACK):
-                if first + n == V:
-                    nc.vector.tensor_scalar(h2[t][:, cols], h2_banks[t][:, cols], SIXTEENTH, None, ALU.mult)
-                else:
-                    nc.scalar.activation(h2[t][:, cols], h2_banks[t][:, cols], ACT.Copy, scale=SIXTEENTH)
-
-        pairs, both = line_up(0, 0, 256, "a")
-        z0 = weave(0, 256, combine(0, 256, pairs, both, "larger", False), "b", False)
-        pairs, both = line_up(1, 256, 128, "a")
-        z1 = weave(1, 128, combine(1, 128, pairs, both, "larger", False), "c", False)
-        second_product(0, 0, 256, z0, 1)
-        empty(0, 256)
-        pairs, both = line_up(2, 384, 128, "b")
-        second_product(1, 256, 128, z1, 1)
-        empty(256, 128)
-        z2 = weave(2, 128, combine(2, 128, pairs, both, "c", True), "d", True)
-        second_product(2, 384, 128, z2, 2)
-        empty(384, 128)
+        z0 = first_chunk(256)
+        pairs, both = line_up(1, 256, 256, "a")
+        second_product("0", 0, z0)
+        for t in range(PACK):
+            empty(t, slice(0, HALF), "scalar")
+        second_chunk(HALF, pairs, both)
+        for t in range(PACK):
+            empty(t, slice(HALF, V), "vector")
 
         out_rows = out.rearrange("(p t) v -> p t v", t=PACK)
 
-        def finish(t, far, near, width):
+        def finish(t, far, near, widths):
             result = keep.tile([P, V], F32, name=f"result{t}", align_bytes=64)
-            for v0 in range(0, V, width):
-                cols = slice(v0, v0 + width)
+            for i, width in enumerate(widths):
+                cols = slice(sum(widths[:i]), sum(widths[:i]) + width)
                 nc.vector.tensor_tensor(result[:, cols], far[:, cols], near[:, cols], ALU.subtract)
                 nc.sync.dma_start(out_rows[:, t, cols], result[:, cols])
 
-        waiting = None
-        for t in range(PACK):
-            gate = keep.tile([P, V], F32, name=f"gate{t}", align_bytes=64)
-            near = keep.tile([P, V], F32, name=f"near{t}", align_bytes=64)
-            far = keep.tile([P, V], F32, name=f"far{t}", align_bytes=64)
+        def add_turned(t, far, faded):
+            turned_bank = psum.tile([P, V], F32, name=f"turned_bank{t}", tag=f"bank{5 + t}")
+            terms = (h2[t], far, faded)
+            for i, term in enumerate(terms):
+                for v0 in range(0, V, P):
+                    cols = slice(v0, v0 + P)
+                    nc.tensor.matmul(
+                        turned_bank[:, cols], term[:, cols], identity[:], is_transpose=True,
+                        start=i == 0 and v0 == 0, stop=i == len(terms) - 1 and v0 == V - P,
+                    )
+            return turned_bank
+
+        def turn_back(t, turned_bank):
+            turned = keep.tile([P, V], F32, name=f"turned{t}", align_bytes=64)
+            nc.scalar.copy(turned[:], turned_bank[:])
+            back_bank = psum.tile([P, V], F32, name=f"back_bank{t}", tag=f"bank{(7 + t) % 8}")
+            for v0 in range(0, V, P):
+                cols = slice(v0, v0 + P)
+                nc.tensor.transpose(back_bank[:, cols], turned[:, cols], identity[:])
+            return back_bank
+
+        def store_back(t, back_bank):
+            result = keep.tile([P, V], F32, name=f"result{t}", align_bytes=64)
+            nc.scalar.copy(result[:], back_bank[:])
+            nc.scalar.dma_start(out_rows[:, t, :], result[:])
+
+        def make_gate(t, tag):
+            gate = keep.tile([P, V], F32, name=f"gate{t}", tag=tag, align_bytes=64)
             for v0 in range(0, V, HALF):
                 cols = slice(v0, v0 + HALF)
                 nc.scalar.activation(gate[:, cols], h2[t][:].indirect(entries(n2_t, v0, HALF)), ACT.Sigmoid)
-            if t > 0:
-                nc.vector.scalar_tensor_tensor(near[:], gate[:], 1.0, h2[t][:], ALU.subtract, ALU.mult)
-                finish(*waiting)
+            return gate
+
+        def blend(t, gate, far_tag):
+            near = keep.tile([P, V], F32, name=f"near{t}", align_bytes=64)
+            far = keep.tile([P, V], F32, name=f"far{t}", tag=far_tag, align_bytes=64)
+            first_op = (-1.0, ALU.mult) if t < TURNED else (1.0, ALU.subtract)
             for v0 in range(0, V, HALF):
                 cols = slice(v0, v0 + HALF)
                 nc.vector.tensor_tensor(far[:, cols], h2[t][:].indirect(entries(n3_t, v0, HALF)), gate[:, cols], ALU.mult)
-                if t == 0:
-                    nc.vector.scalar_tensor_tensor(near[:, cols], gate[:, cols], 1.0, h2[t][:, cols], ALU.subtract, ALU.mult)
-            waiting = (t, far, near, HALF if t == PACK - 1 else V)
-        finish(*waiting)
+            nc.vector.scalar_tensor_tensor(near[:], gate[:], first_op[0], h2[t][:], first_op[1], ALU.mult)
+            return far, near
+
+        gates = [make_gate(t, f"gate{t}") for t in range(PACK)]
+        gate3 = gates[3]
+        turned = [add_turned(t, *blend(t, gates[t], f"far{t}")) for t in range(TURNED)]
+        backs = [turn_back(t, turned[t]) for t in range(TURNED)]
+        for t in range(TURNED):
+            store_back(t, backs[t])
+        far2, near2 = blend(2, gates[2], "far2")
+        near3 = keep.tile([P, V], F32, name="near3", align_bytes=64)
+        far3 = keep.tile([P, V], F32, name="far3", align_bytes=64)
+        nc.vector.scalar_tensor_tensor(near3[:], gate3[:], 1.0, h2[3][:], ALU.subtract, ALU.mult)
+        finish(2, far2, near2, (V,))
+        for v0 in range(0, V, HALF):
+            cols = slice(v0, v0 + HALF)
+            nc.vector.tensor_tensor(far3[:, cols], h2[3][:].indirect(entries(n3_t, v0, HALF)), gate3[:, cols], ALU.mult)
+        finish(3, far3, near3, (256, 128, 128))

@@ -51,6 +51,11 @@ def tile_picked_ringpgaptrack_none_p_kernel(tc, x_words, x_scales, d_words, d_sc
         nc.vector.memset(x_bytes[:].bitcast(I32), 0)
         nc.vector.memset(w_scales[:].bitcast(I32), 0)
 
+        warm_in = keep.tile([P, 1], F32, name="warm_in")
+        warm_out = keep.tile([P, 1], F32, name="warm_out")
+        nc.vector.memset(warm_in[:], 0.0)
+        nc.scalar.activation(warm_out[:], warm_in[:], ACT.Sigmoid)
+
         nc.sync.dma_start(k1_t[:], k1)
         nc.sync.dma_start(d_bytes[:].bitcast(I32)[0:P:8, :], d_scales[0].bitcast(I32))
         nc.sync.dma_start(offs_t[:], offs)
@@ -112,7 +117,7 @@ def tile_picked_ringpgaptrack_none_p_kernel(tc, x_words, x_scales, d_words, d_sc
                 nc.scalar.activation(h[t][:, cols], bank[:], ACT.Copy, scale=SIXTEENTH / 2)
 
         h2 = [keep.tile([P, V], F32, name=f"h2_{t}", align_bytes=64) for t in range(PACK)]
-        h2_banks = [psum.tile([P, V], F32, name=f"h2_bank{t}", tag=f"bank{t + 1}") for t in range(PACK)]
+        h2_banks = {}
 
         def line_up(c, first, n, tag):
             lined = keep.tile([P, PACK * 2 * n], F32, name=f"lined{c}", tag=tag, align_bytes=64)
@@ -127,9 +132,9 @@ def tile_picked_ringpgaptrack_none_p_kernel(tc, x_words, x_scales, d_words, d_sc
 
         def empty(t, cols, engine):
             if engine == "vector":
-                nc.vector.tensor_scalar(h2[t][:, cols], h2_banks[t][:, cols], SIXTEENTH, None, ALU.mult)
+                nc.vector.tensor_scalar(h2[t][:, cols], h2_banks[cols.start][t][:], SIXTEENTH, None, ALU.mult)
             else:
-                nc.scalar.activation(h2[t][:, cols], h2_banks[t][:, cols], ACT.Copy, scale=SIXTEENTH)
+                nc.scalar.activation(h2[t][:, cols], h2_banks[cols.start][t][:], ACT.Copy, scale=SIXTEENTH)
 
         def second_product(name, first, z):
             n = z.shape[1] // PACK
@@ -137,7 +142,7 @@ def tile_picked_ringpgaptrack_none_p_kernel(tc, x_words, x_scales, d_words, d_sc
             z_scales = keep.tile([P, n], U8, name=f"z_scales{name}", align_bytes=64)
             nc.vector.quantize_mx(z_words[:].bitcast(FP8X4), z_scales[:], z[:])
             for t in range(PACK):
-                product(h2_banks[t][:, first : first + n], t, z_words[:], z_scales[:])
+                product(h2_banks[first // HALF * HALF][t][:, first % HALF : first % HALF + n], t, z_words[:], z_scales[:])
 
         def second_chunk(n, pairs, both):
             m = n // 2
@@ -147,21 +152,28 @@ def tile_picked_ringpgaptrack_none_p_kernel(tc, x_words, x_scales, d_words, d_sc
             by_plane = pairs.rearrange("p (t v) e -> p t v e", t=PACK)
             both_planes = both[:].rearrange("p (t v) -> p t v", t=PACK)
             larger = [keep.tile([P, PACK, m], F32, name=f"larger{i}", align_bytes=64) for i in range(2)]
-            gap = [keep.tile([P, PACK, m], F32, name=f"gap{i}", tag=("gap0", "z0")[i], align_bytes=64) for i in range(2)]
-            z = [keep.tile([P, PACK * m], BF16, name=f"z1_{i}", align_bytes=64) for i in range(2)]
+            gap = [keep.tile([P, PACK, m], F32, name=f"gap{i}", align_bytes=64) for i in range(2)]
             for i in range(2):
                 nc.vector.tensor_tensor(larger[i][:], by_plane[:, :, halves[i], 0], by_plane[:, :, halves[i], 1], ALU.max)
             for i in range(2):
                 nc.vector.scalar_tensor_tensor(gap[i][:], larger[i][:], 3.0, both_planes[:, :, halves[i]], ALU.mult, ALU.subtract)
-            for i in range(2):
-                nc.vector.tensor_tensor(
-                    z[i][:].rearrange("p (c i t) -> p c t i", i=4, t=PACK),
-                    gap[i][:].rearrange("p t (c i) -> p c t i", i=4),
-                    gain[:].rearrange("p (c t i) -> p c t i", c=1, i=1).to_broadcast([P, m // 4, PACK, 4]),
-                    ALU.mult,
-                )
-            for i in range(2):
-                second_product(f"1_{i}", n + m * i, z[i])
+            planes = keep.tile([P, PACK, m], BF16, name="planes1", tag="planes", align_bytes=64)
+            for t in range(PACK):
+                nc.scalar.activation(planes[:, t, :], gap[0][:, t, :], ACT.Copy, scale=gain[:, t : t + 1])
+            z_low = keep.tile([P, PACK * m], BF16, name="z_low", align_bytes=64)
+            nc.scalar.copy(z_low[:].rearrange("p (c i t) -> p c t i", i=4, t=PACK), planes[:].rearrange("p t (c i) -> p c t i", i=4))
+            second_product("0", 0, z0)
+            for t in range(PACK):
+                empty(t, slice(0, HALF), "scalar")
+            z_high = keep.tile([P, PACK * m], BF16, name="z_high", tag="z0", align_bytes=64)
+            nc.vector.tensor_tensor(
+                z_high[:].rearrange("p (c i t) -> p c t i", i=4, t=PACK),
+                gap[1][:].rearrange("p t (c i) -> p c t i", i=4),
+                gain[:].rearrange("p (c t i) -> p c t i", c=1, i=1).to_broadcast([P, m // 4, PACK, 4]),
+                ALU.mult,
+            )
+            second_product("high", n + m, z_high)
+            second_product("low", n, z_low)
 
         def first_chunk(n):
             half_gain = keep.tile([P, PACK], F32, name="half_gain")
@@ -208,10 +220,9 @@ def tile_picked_ringpgaptrack_none_p_kernel(tc, x_words, x_scales, d_words, d_sc
             return z
 
         z0 = first_chunk(256)
+        h2_banks[0] = [psum.tile([P, HALF], F32, name=f"h2_bank0_{t}", tag=f"bank{t + 1}") for t in range(PACK)]
+        h2_banks[HALF] = [psum.tile([P, HALF], F32, name=f"h2_bank1_{t}", tag=f"bank{(t + 5) % 8}") for t in range(PACK)]
         pairs, both = line_up(1, 256, 256, "a")
-        second_product("0", 0, z0)
-        for t in range(PACK):
-            empty(t, slice(0, HALF), "scalar")
         second_chunk(HALF, pairs, both)
         for t in range(PACK):
             empty(t, slice(HALF, V), "vector")
@@ -226,7 +237,7 @@ def tile_picked_ringpgaptrack_none_p_kernel(tc, x_words, x_scales, d_words, d_sc
                 nc.sync.dma_start(out_rows[:, t, cols], result[:, cols])
 
         def add_turned(t, far, faded):
-            turned_bank = psum.tile([P, V], F32, name=f"turned_bank{t}", tag=f"bank{5 + t}")
+            turned_bank = psum.tile([P, V], F32, name=f"turned_bank{t}", tag=f"bank{1 + t}")
             terms = (h2[t], far, faded)
             for i, term in enumerate(terms):
                 for v0 in range(0, V, P):
@@ -240,7 +251,7 @@ def tile_picked_ringpgaptrack_none_p_kernel(tc, x_words, x_scales, d_words, d_sc
         def turn_back(t, turned_bank):
             turned = keep.tile([P, V], F32, name=f"turned{t}", align_bytes=64)
             nc.scalar.copy(turned[:], turned_bank[:])
-            back_bank = psum.tile([P, V], F32, name=f"back_bank{t}", tag=f"bank{(7 + t) % 8}")
+            back_bank = psum.tile([P, V], F32, name=f"back_bank{t}", tag=f"bank{3 + t}")
             for v0 in range(0, V, P):
                 cols = slice(v0, v0 + P)
                 nc.tensor.transpose(back_bank[:, cols], turned[:, cols], identity[:])

from contextlib import ExitStack

import concourse.mybir as mybir
from concourse.masks import make_identity

K, T, S, V, G, H = 512, 2048, 1024, 512, 2048, 512
FLOPS = 2 * K * H * (S + V)

F32 = mybir.dt.float32
BF16 = mybir.dt.bfloat16
I32 = mybir.dt.int32
U32 = mybir.dt.uint32
U16 = mybir.dt.uint16
U8 = mybir.dt.uint8
FP8X4 = mybir.dt.float8_e4m3fn_x4
ALU = mybir.AluOpType
ACT = mybir.ActivationFunctionType

P = 128
PACK = 4
BANK = 512
SIXTEENTH = 0.0625
PAIR_CHUNKS = (256, 128, 128)
HALF = V // 2
TURNED = 2


def entries(lists, first, count):
    return lists[:, first // 16 : (first + count) // 16]


def tile_picked_ringpgaptrack_none_p_kernel(tc, x_words, x_scales, d_words, d_scales, gs, offs, k1, n1, n2, n3, out):
    nc = tc.nc
    with ExitStack() as ctx:
        keep = ctx.enter_context(tc.tile_pool(name="keep", bufs=1))
        psum = ctx.enter_context(tc.psum_pool(name="psum", bufs=1))

        k1_t = keep.tile([P, H // 16], U16, name="k1_t")
        offs_t = keep.tile([P, S // 16], U16, name="offs_t")
        n1_t = keep.tile([P, S // 16], U16, name="n1_t")
        n2_t = keep.tile([P, V // 16], U16, name="n2_t")
        n3_t = keep.tile([P, V // 16], U16, name="n3_t")
        gain = keep.tile([P, PACK], F32, name="gain")
        d_bytes = keep.tile([P, G], U8, name="d_bytes", align_bytes=64)
        x_bytes = keep.tile([P, T], U8, name="x_bytes", align_bytes=64)
        d_table = keep.tile([P, G], U32, name="d_table", align_bytes=64)
        x_table = keep.tile([P, T], U32, name="x_table", align_bytes=64)
        w_scales = keep.tile([P, H], U8, name="w_scales", align_bytes=64)

        nc.vector.memset(d_bytes[:].bitcast(I32), 0)
        nc.vector.memset(x_bytes[:].bitcast(I32), 0)
        nc.vector.memset(w_scales[:].bitcast(I32), 0)

        warm_in = keep.tile([P, 1], F32, name="warm_in")
        warm_out = keep.tile([P, 1], F32, name="warm_out")
        nc.vector.memset(warm_in[:], 0.0)
        nc.scalar.activation(warm_out[:], warm_in[:], ACT.Sigmoid)

        nc.sync.dma_start(k1_t[:], k1)
        nc.sync.dma_start(d_bytes[:].bitcast(I32)[0:P:8, :], d_scales[0].bitcast(I32))
        nc.sync.dma_start(offs_t[:], offs)
        for q in range(4):
            nc.sync.dma_start(x_bytes[:].bitcast(I32)[32 * q : 32 * q + 4, :], x_scales[0, 4 * q : 4 * q + 4, :].bitcast(I32))
        nc.sync.dma_start(d_table[:].bitcast(I32), d_words[0].rearrange("p n t -> p (n t)").bitcast(I32))
        nc.sync.dma_start(x_table[:].bitcast(I32), x_words[0].rearrange("p n t -> p (n t)").bitcast(I32))
        nc.sync.dma_start(n1_t[:], n1)

        xq_scales = keep.tile([P, S], U8, name="xq_scales", align_bytes=64)
        xq_words = keep.tile([P, S], U32, name="xq_words", align_bytes=64)

        def pick_x(table, picked, first, n):
            nc.vector.tensor_copy(picked[:, first : first + n], table[:].indirect(entries(offs_t, first, n)))

        picked_d_bytes = keep.tile([P, H], U8, name="picked_d_bytes", align_bytes=64)
        nc.vector.tensor_copy(picked_d_bytes[:], d_bytes[:].indirect(k1_t[:]))
        pick_x(x_bytes, xq_scales, 0, 512)
        dealt_d_bytes = keep.tile([P, H], U8, name="dealt_d_bytes", align_bytes=64)
        nc.vector.tensor_copy(
            dealt_d_bytes[:].rearrange("p (t m) -> p m t", t=PACK), picked_d_bytes[:].rearrange("p (m t) -> p m t", t=PACK)
        )
        for j in range(4):
            nc.scalar.dma_start(w_scales[:].bitcast(I32)[j:P:32, :], dealt_d_bytes[:].bitcast(I32)[8 * j : P : 32, :])

        nc.sync.dma_start(gain[:], gs.rearrange("(p t) o -> p (t o)", t=PACK))
        nc.sync.dma_start(n2_t[:], n2)
        nc.sync.dma_start(n3_t[:], n3)

        picked_d_words = keep.tile([P, H], U32, name="picked_d_words", tag="picked_d_words", align_bytes=64)
        nc.vector.tensor_copy(picked_d_words[:], d_table[:].indirect(k1_t[:]))
        pick_x(x_bytes, xq_scales, 512, 512)
        w_words = keep.tile([P, H], U32, name="w_words", align_bytes=64)
        nc.vector.tensor_copy(
            w_words[:].rearrange("p (t m) -> p m t", t=PACK), picked_d_words[:].rearrange("p (m t) -> p m t", t=PACK)
        )

        def product(bank, t, codes, scales):
            cols = slice(P * t, P * (t + 1))
            nc.tensor.matmul_mx(
                bank, lhsT=w_words[:, cols].bitcast(FP8X4), lhsT_scale=w_scales[:, cols],
                rhs=codes.bitcast(FP8X4), rhs_scale=scales, start=True, stop=True,
            )

        identity = keep.tile([P, P], F32, name="identity", tag="picked_d_words", align_bytes=64)
        make_identity(nc, identity[:])
        h = [keep.tile([P, S], F32, name=f"h{t}", align_bytes=64) for t in range(PACK)]
        pick_x(x_table, xq_words, 0, 512)
        pick_x(x_table, xq_words, 512, 256)
        pick_x(x_table, xq_words, 768, 256)
        steps = ((0, 0, 512), (0, 512, 256), (0, 768, 256), (1, 0, 512), (1, 512, 512), (2, 0, 512), (2, 512, 512), (3, 0, 512), (3, 512, 512))
        for i, (t, first, n) in enumerate(steps):
            bank = psum.tile([P, n], F32, name=f"h_bank{i}", tag=f"bank{i % 8}")
            cols = slice(first, first + n)
            product(bank[:], t, xq_words[:, cols], xq_scales[:, cols])
            if i == 2:
                nc.vector.tensor_scalar(h[t][:, cols], bank[:], SIXTEENTH / 2, None, ALU.mult)
            else:
                nc.scalar.activation(h[t][:, cols], bank[:], ACT.Copy, scale=SIXTEENTH / 2)

        h2 = [keep.tile([P, V], F32, name=f"h2_{t}", align_bytes=64) for t in range(PACK)]
        h2_banks = {}

        def line_up(c, first, n, tag):
            lined = keep.tile([P, PACK * 2 * n], F32, name=f"lined{c}", tag=tag, align_bytes=64)
            pairs = lined[:].rearrange("p (v e) -> p v e", e=2)
            both = keep.tile([P, PACK * n], F32, name=f"both{c}", align_bytes=64)
            for t in range(PACK):
                nc.vector.tensor_copy(lined[:, 2 * n * t : 2 * n * (t + 1)], h[t][:].indirect(entries(n1_t, 2 * first, 2 * n)))
                if t < PACK - 1:
                    cols = slice(n * t, n * (t + 1))
                    nc.gpsimd.tensor_tensor(both[:, cols], pairs[:, cols, 0], pairs[:, cols, 1], ALU.add)
            return pairs, both

        def empty(t, cols, engine):
            if engine == "vector":
                nc.vector.tensor_scalar(h2[t][:, cols], h2_banks[cols.start][t][:], SIXTEENTH, None, ALU.mult)
            else:
                nc.scalar.activation(h2[t][:, cols], h2_banks[cols.start][t][:], ACT.Copy, scale=SIXTEENTH)

        def second_product(name, first, z):
            n = z.shape[1] // PACK
            z_words = keep.tile([P, n], U32, name=f"z_words{name}", align_bytes=64)
            z_scales = keep.tile([P, n], U8, name=f"z_scales{name}", align_bytes=64)
            nc.vector.quantize_mx(z_words[:].bitcast(FP8X4), z_scales[:], z[:])
            for t in range(PACK):
                product(h2_banks[first // HALF * HALF][t][:, first % HALF : first % HALF + n], t, z_words[:], z_scales[:])

        def second_chunk(n, pairs, both):
            m = n // 2
            halves = (slice(0, m), slice(m, n))
            tail = slice(n * (PACK - 1), n * PACK)
            nc.vector.tensor_tensor(both[:, tail], pairs[:, tail, 0], pairs[:, tail, 1], ALU.add)
            by_plane = pairs.rearrange("p (t v) e -> p t v e", t=PACK)
            both_planes = both[:].rearrange("p (t v) -> p t v", t=PACK)
            larger = [keep.tile([P, PACK, m], F32, name=f"larger{i}", align_bytes=64) for i in range(2)]
            gap = [keep.tile([P, PACK, m], F32, name=f"gap{i}", align_bytes=64) for i in range(2)]
            for i in range(2):
                nc.vector.tensor_tensor(larger[i][:], by_plane[:, :, halves[i], 0], by_plane[:, :, halves[i], 1], ALU.max)
            for i in range(2):
                nc.vector.scalar_tensor_tensor(gap[i][:], larger[i][:], 3.0, both_planes[:, :, halves[i]], ALU.mult, ALU.subtract)
            planes = keep.tile([P, PACK, m], BF16, name="planes1", tag="planes", align_bytes=64)
            for t in range(PACK):
                nc.scalar.activation(planes[:, t, :], gap[0][:, t, :], ACT.Copy, scale=gain[:, t : t + 1])
            z_low = keep.tile([P, PACK * m], BF16, name="z_low", align_bytes=64)
            nc.scalar.copy(z_low[:].rearrange("p (c i t) -> p c t i", i=4, t=PACK), planes[:].rearrange("p t (c i) -> p c t i", i=4))
            second_product("0", 0, z0)
            for t in range(PACK):
                empty(t, slice(0, HALF), "scalar")
            z_high = keep.tile([P, PACK * m], BF16, name="z_high", tag="z0", align_bytes=64)
            nc.vector.tensor_tensor(
                z_high[:].rearrange("p (c i t) -> p c t i", i=4, t=PACK),
                gap[1][:].rearrange("p t (c i) -> p c t i", i=4),
                gain[:].rearrange("p (c t i) -> p c t i", c=1, i=1).to_broadcast([P, m // 4, PACK, 4]),
                ALU.mult,
            )
            second_product("high", n + m, z_high)
            second_product("low", n, z_low)

        def first_chunk(n):
            half_gain = keep.tile([P, PACK], F32, name="half_gain")
            nc.scalar.activation(half_gain[:], gain[:], ACT.Copy, scale=0.5)
            lined = keep.tile([P, PACK * 2 * n], F32, name="lined0", align_bytes=64)
            pairs = lined[:].rearrange("p (v e) -> p v e", e=2)
            spread = keep.tile([P, PACK * n], F32, name="spread", align_bytes=64)
            sum_banks = [psum.tile([P, BANK], F32, name=f"sum_bank{j}", tag=f"bank{5 + j}") for j in range(n // P)]
            for t in range(PACK):
                nc.vector.tensor_copy(lined[:, 2 * n * t : 2 * n * (t + 1)], h[t][:].indirect(entries(n1_t, 0, 2 * n)))
                cols = slice(n * t, n * (t + 1))
                apart = keep.tile([P, n], F32, name=f"apart{t}", tag="a" if t == 0 else f"apart{t}", align_bytes=64)
                nc.gpsimd.tensor_tensor(apart[:], pairs[:, cols, 0], pairs[:, cols, 1], ALU.subtract)
                nc.scalar.activation(spread[:, cols], apart[:], ACT.Abs, scale=3.0)
            for t in range(PACK):
                for j in range(n // P):
                    cols = slice(n * t + P * j, n * t + P * (j + 1))
                    for e in range(2):
                        nc.tensor.matmul(
                            sum_banks[j][:, P * t : P * (t + 1)], pairs[:, cols, e], identity[:], is_transpose=True,
                            start=t == 0 and e == 0, stop=False,
                        )
                for u in ([t - 1] if 0 < t < PACK - 1 else [t - 1, t] if t > 0 else []):
                    for j in range(n // P):
                        cols = slice(n * u + P * j, n * u + P * (j + 1))
                        nc.tensor.matmul(
                            sum_banks[j][:, P * u : P * (u + 1)], spread[:, cols], identity[:], is_transpose=True,
                            start=False, stop=u == PACK - 1,
                        )
            turned = keep.tile([P, PACK * n], F32, name="turned_gap", align_bytes=64)
            back_banks = [psum.tile([P, BANK], F32, name=f"gap_bank{j}", tag=f"bank{(7 + j) % 8}") for j in range(2)]
            for j in range(n // P):
                nc.scalar.copy(turned[:, BANK * j : BANK * (j + 1)], sum_banks[j][:])
            for j in range(n // P):
                for t in range(PACK):
                    place = n * (t % 2) + P * j
                    nc.tensor.transpose(back_banks[t // 2][:, place : place + P], turned[:, BANK * j + P * t : BANK * j + P * (t + 1)], identity[:])
            planes = keep.tile([P, PACK * n], BF16, name="planes0", tag="planes", align_bytes=64)
            for t in range(PACK):
                place = n * (t % 2)
                nc.scalar.activation(planes[:, n * t : n * (t + 1)], back_banks[t // 2][:, place : place + n], ACT.Copy, scale=half_gain[:, t : t + 1])
            z = keep.tile([P, PACK * n], BF16, name="z0", tag="z0", align_bytes=64)
            nc.scalar.copy(z[:].rearrange("p (c i t) -> p c t i", i=4, t=PACK), planes[:].rearrange("p (t c i) -> p c t i", t=PACK, i=4))
            return z

        z0 = first_chunk(256)
        h2_banks[0] = [psum.tile([P, HALF], F32, name=f"h2_bank0_{t}", tag=f"bank{t + 1}") for t in range(PACK)]
        h2_banks[HALF] = [psum.tile([P, HALF], F32, name=f"h2_bank1_{t}", tag=f"bank{(t + 5) % 8}") for t in range(PACK)]
        pairs, both = line_up(1, 256, 256, "a")
        second_chunk(HALF, pairs, both)
        for t in range(PACK):
            empty(t, slice(HALF, V), "vector")

        out_rows = out.rearrange("(p t) v -> p t v", t=PACK)

        def finish(t, far, near, widths):
            result = keep.tile([P, V], F32, name=f"result{t}", align_bytes=64)
            for i, width in enumerate(widths):
                cols = slice(sum(widths[:i]), sum(widths[:i]) + width)
                nc.vector.tensor_tensor(result[:, cols], far[:, cols], near[:, cols], ALU.subtract)
                nc.sync.dma_start(out_rows[:, t, cols], result[:, cols])

        def add_turned(t, far, faded):
            turned_bank = psum.tile([P, V], F32, name=f"turned_bank{t}", tag=f"bank{1 + t}")
            terms = (h2[t], far, faded)
            for i, term in enumerate(terms):
                for v0 in range(0, V, P):
                    cols = slice(v0, v0 + P)
                    nc.tensor.matmul(
                        turned_bank[:, cols], term[:, cols], identity[:], is_transpose=True,
                        start=i == 0 and v0 == 0, stop=i == len(terms) - 1 and v0 == V - P,
                    )
            return turned_bank

        def turn_back(t, turned_bank):
            turned = keep.tile([P, V], F32, name=f"turned{t}", align_bytes=64)
            nc.scalar.copy(turned[:], turned_bank[:])
            back_bank = psum.tile([P, V], F32, name=f"back_bank{t}", tag=f"bank{3 + t}")
            for v0 in range(0, V, P):
                cols = slice(v0, v0 + P)
                nc.tensor.transpose(back_bank[:, cols], turned[:, cols], identity[:])
            return back_bank

        def store_back(t, back_bank):
            result = keep.tile([P, V], F32, name=f"result{t}", align_bytes=64)
            nc.scalar.copy(result[:], back_bank[:])
            nc.scalar.dma_start(out_rows[:, t, :], result[:])

        def make_gate(t, tag):
            gate = keep.tile([P, V], F32, name=f"gate{t}", tag=tag, align_bytes=64)
            for v0 in range(0, V, HALF):
                cols = slice(v0, v0 + HALF)
                nc.scalar.activation(gate[:, cols], h2[t][:].indirect(entries(n2_t, v0, HALF)), ACT.Sigmoid)
            return gate

        def blend(t, gate, far_tag):
            near = keep.tile([P, V], F32, name=f"near{t}", align_bytes=64)
            far = keep.tile([P, V], F32, name=f"far{t}", tag=far_tag, align_bytes=64)
            first_op = (-1.0, ALU.mult) if t < TURNED else (1.0, ALU.subtract)
            for v0 in range(0, V, HALF):
                cols = slice(v0, v0 + HALF)
                nc.vector.tensor_tensor(far[:, cols], h2[t][:].indirect(entries(n3_t, v0, HALF)), gate[:, cols], ALU.mult)
            nc.vector.scalar_tensor_tensor(near[:], gate[:], first_op[0], h2[t][:], first_op[1], ALU.mult)
            return far, near

        gates = [make_gate(t, f"gate{t}") for t in range(PACK)]
        gate3 = gates[3]
        turned = [add_turned(t, *blend(t, gates[t], f"far{t}")) for t in range(TURNED)]
        backs = [turn_back(t, turned[t]) for t in range(TURNED)]
        for t in range(TURNED):
            store_back(t, backs[t])
        far2, near2 = blend(2, gates[2], "far2")
        near3 = keep.tile([P, V], F32, name="near3", align_bytes=64)
        far3 = keep.tile([P, V], F32, name="far3", align_bytes=64)
        nc.vector.scalar_tensor_tensor(near3[:], gate3[:], 1.0, h2[3][:], ALU.subtract, ALU.mult)
        finish(2, far2, near2, (V,))
        for v0 in range(0, V, HALF):
            cols = slice(v0, v0 + HALF)
            nc.vector.tensor_tensor(far3[:, cols], h2[3][:].indirect(entries(n3_t, v0, HALF)), gate3[:, cols], ALU.mult)
        finish(3, far3, near3, (256, 128, 128))
